import numpy as np
import ml_dtypes


def mxq(x, axis, fmt="e4m3"):
    dtype, down = {"e4m3": (ml_dtypes.float8_e4m3fn, 7), "e5m2": (ml_dtypes.float8_e5m2, 14)}[fmt]
    v = np.moveaxis(np.asarray(x, np.float32).astype(ml_dtypes.bfloat16).astype(np.float64), axis, -1)
    blocks = v.reshape(v.shape[:-1] + (-1, 32))
    amax = np.abs(blocks).max(-1, keepdims=True)
    byte = np.maximum(np.where(amax > 0, np.frexp(amax)[1] - 1 + 127, 0) - down, 1)
    scale = np.exp2(byte - 127.0)
    codes = (blocks / scale).astype(np.float32).astype(dtype).astype(np.float64)
    return np.moveaxis((codes * scale).reshape(v.shape), -1, axis)


WIDE = False


def mx_kscale(k):
    if not WIDE:
        return np.ones(k)
    levels = np.array([10, -10, 5, -5, 0])
    if k % 512:
        return np.exp2(np.random.permutation(np.resize(levels, k // 32))).repeat(32)
    a = np.empty((k // 512, 16))
    for p in range(k // 512):
        a[p, :8] = np.random.permutation(np.resize(levels, 8))
        for g in range(8):
            far = levels[np.abs(levels - a[p, g]) >= 10]
            a[p, g + 8] = far[np.random.randint(len(far))]
    return np.exp2(a.ravel()).repeat(32)


def f64(x):
    return np.asarray(x).astype(np.float64)


E2M1 = np.array([0.0, 0.5, 1.0, 1.5, 2.0, 3.0, 4.0, 6.0, -0.0, -0.5, -1.0, -1.5, -2.0, -3.0, -4.0, -6.0])


def pack_weight(w, fmt):
    k, n = w.shape
    w = f64(np.asarray(w, np.float32).astype(ml_dtypes.bfloat16)).reshape(k // 32, 32, n)
    amax = np.abs(w).max(1)
    if fmt == "e4m3":
        byte = np.frexp(amax)[1] - 1 + 127 - 7
    else:
        mant, ex = np.frexp(amax / 6.0)
        byte = np.where(mant > 0.5, ex, ex - 1) + 127
    byte = np.clip(np.where(amax > 0, byte, 1), 1, 254)
    scaled = (w * np.exp2(127.0 - byte)[:, None, :]).reshape(k, n).astype(np.float32)
    by_word = np.ascontiguousarray(scaled.reshape(k // 512, 128, 4, n).transpose(0, 1, 3, 2))
    if fmt == "e4m3":
        words = by_word.astype(ml_dtypes.float8_e4m3fn).view(np.uint8)
    else:
        c = by_word.astype(ml_dtypes.float4_e2m1fn).view(np.uint8) & 0xF
        words = (c[..., 0::2] | (c[..., 1::2] << 4)).reshape(k // 512, 128, 2 * n)
    return np.ascontiguousarray(words), np.ascontiguousarray(byte.astype(np.uint8).reshape(k // 512, 16, n))


def unpack_weight(words, scales, fmt):
    g, _, n = scales.shape
    words = np.ascontiguousarray(words).reshape(g, 128, n, -1)
    if fmt == "e4m3":
        vals = words.view(ml_dtypes.float8_e4m3fn).astype(np.float64)
    else:
        nib = np.empty((g, 128, n, 4), np.uint8)
        nib[..., 0::2] = words & 0xF
        nib[..., 1::2] = words >> 4
        vals = E2M1[nib]
    vals = vals * np.repeat(np.exp2(scales.astype(np.float64) - 127.0), 8, axis=1)[..., None]
    return vals.transpose(0, 1, 3, 2).reshape(g * 512, n)


O, K, R, M, T = 1024, 2048, 512, 1536, 512


def setup_inputs():
    n = np.random.standard_normal
    s = mx_kscale(K)[:, None]
    u = mx_kscale(R)[:, None]
    x = n((K, T)); x[:O] *= 6.0
    w = n((K, M)) / np.sqrt(K) / s; w[:O] /= 2.0
    p_w8 = pack_weight(w[:O], "e4m3")
    p_w4 = pack_weight(w[O:], "e2m1")
    p_up = pack_weight(n((R, M)) / np.sqrt(R) / u, "e2m1")
    return {
        "x": (x * s).astype(np.float32),
        "w8_words": p_w8[0],
        "w8_scales": p_w8[1],
        "w4_words": p_w4[0],
        "w4_scales": p_w4[1],
        "down": (0.3 * n((K, R)) / np.sqrt(K) / s * u.T).astype(np.float32),
        "up_words": p_up[0],
        "up_scales": p_up[1],
    }


def reference(x, w8_words, w8_scales, w4_words, w4_scales, down, up_words, up_scales):
    x_ = mxq(f64(x), 0, "e4m3")
    w8_ = unpack_weight(w8_words, w8_scales, "e4m3")
    w4_ = unpack_weight(w4_words, w4_scales, "e2m1")
    down_ = mxq(f64(down), 0, "e4m3")
    up_ = unpack_weight(up_words, up_scales, "e2m1")
    h_ = mxq(down_.T @ x_, 0, "e4m3")
    y = w8_.T @ x_[:O] + w4_.T @ x_[O:] + up_.T @ h_
    return y

@@ -1,0 +1,211 @@
+from contextlib import ExitStack
+
+import concourse.mybir as mybir
+
+K, T, R, M = 2048, 512, 512, 1536
+FLOPS = 2 * (K * R * T + K * M * T + R * M * T)
+
+F32 = mybir.dt.float32
+BF16 = mybir.dt.bfloat16
+I32 = mybir.dt.int32
+U32 = mybir.dt.uint32
+U8 = mybir.dt.uint8
+FP8X4 = mybir.dt.float8_e4m3fn_x4
+FP4X4 = mybir.dt.float4_e2m1fn_x4
+
+P = 128
+PACK = 4
+G = 512
+X_VEC = 336
+D_VEC = 88
+H_VEC = 344
+
+
+def tile_mix_three_fm_none_kernel(
+    tc, x, w8_words, w8_scales, w4_words, w4_scales, down, up_words, up_scales, out
+):
+    nc = tc.nc
+    with ExitStack() as ctx:
+        keep = ctx.enter_context(tc.tile_pool(name="keep", bufs=1))
+        psum = ctx.enter_context(tc.psum_pool(name="psum", bufs=1))
+        ctx.enter_context(tc.manual_schedule())
+
+        def sb(name, shape, dtype):
+            return keep.tile(shape, dtype, name=name, align_bytes=64)
+
+        planes0 = sb("planes0", [P, 4, G], U8)
+        planes1 = sb("planes1", [P, 4, M - G], U8)
+        up_plane = sb("up_plane", [P, M], U8)
+        warm_in = sb("warm_in", [P, 1], F32)
+        warm_out = sb("warm_out", [P, 1], F32)
+        nc.vector.memset(planes0[:].rearrange("p a n -> p (a n)").bitcast(I32), 0)
+        nc.vector.memset(warm_in[:], 0.0)
+        nc.vector.memset(planes1[:].rearrange("p a n -> p (a n)").bitcast(I32), 0)
+        nc.vector.memset(up_plane[:].bitcast(I32), 0)
+        nc.scalar.copy(warm_out[:], warm_in[:])
+
+        w8_rows = w8_scales.rearrange("a (q r) n -> r q a n", r=4)
+        w4_rows = w4_scales.rearrange("a (q r) n -> r q a n", r=4)
+        up_rows = up_scales.rearrange("a (q r) n -> r q a n", r=4)
+
+        def load_scales(queue, plane, rows, r, cols):
+            queue.dma_start(out=plane[r:P:32].bitcast(I32), in_=rows[r][:, :, cols].bitcast(I32))
+
+        x_raw = [sb(f"x_raw{c}", [P, PACK, T], F32) for c in range(4)]
+        d_raw = [sb(f"d_raw{c}", [P, PACK, R], F32) for c in range(3)]
+        d_raw_half = [sb(f"d_rawh{i}", [P, PACK, R // 2], F32) for i in range(2)]
+        w8_t = [sb(f"w8_{g}", [P, 2, G], U32) for g in range(3)]
+        w4_t = [sb(f"w4_{g}", [P, 2, 2 * G], U8) for g in range(3)]
+        up_t = sb("up_t", [P, 2 * M], U8)
+        w8_view = w8_words.rearrange("a p n i -> p a (n i)")
+        w4_view = w4_words.rearrange("a p b -> p a b")
+
+        def load_k(tile, src, c, cols):
+            rows = src[512 * c : 512 * (c + 1), :].rearrange("(p j) w -> p j w", j=PACK)
+            nc.sync.dma_start(out=tile[:], in_=rows[:, :, cols])
+
+        def load_w(g):
+            nc.sync.dma_start(out=w8_t[g][:].bitcast(I32), in_=w8_view[:, :, 4 * G * g : 4 * G * (g + 1)].bitcast(I32))
+            nc.sync.dma_start(out=w4_t[g][:].bitcast(I32), in_=w4_view[:, :, 2 * G * g : 2 * G * (g + 1)].bitcast(I32))
+
+        load_k(x_raw[0], x, 0, slice(0, T))
+        load_k(x_raw[1], x, 1, slice(0, T))
+        for r in range(4):
+            load_scales(nc.sync, planes0[:, 0:2, :], w8_rows, r, slice(0, G))
+        load_k(x_raw[2], x, 2, slice(0, T))
+        load_k(x_raw[3], x, 3, slice(0, T))
+        for r in range(2):
+            load_scales(nc.sync, planes0[:, 2:4, :], w4_rows, r, slice(0, G))
+        load_w(0)
+        for r in range(2, 4):
+            load_scales(nc.sync, planes0[:, 2:4, :], w4_rows, r, slice(0, G))
+        for c in range(3):
+            load_k(d_raw[c], down, c, slice(0, R))
+        for i in range(2):
+            load_k(d_raw_half[i], down, 3, slice(256 * i, 256 * (i + 1)))
+        load_w(1)
+        for r in range(4):
+            load_scales(nc.sync, planes1[:, 0:2, :], w8_rows, r, slice(G, M))
+        for r in range(4):
+            load_scales(nc.sync, planes1[:, 2:4, :], w4_rows, r, slice(G, M))
+        for r in range(4):
+            nc.sync.dma_start(out=up_plane[r:P:32, :].bitcast(I32), in_=up_rows[r][:, 0, :].bitcast(I32))
+        nc.sync.dma_start(out=up_t[:].bitcast(I32), in_=up_words[0].bitcast(I32))
+        load_w(2)
+
+        x_q = [sb(f"x_q{c}", [P, T], U32) for c in range(4)]
+        x_s = [sb(f"x_s{c}", [P, T], U8) for c in range(4)]
+        x_b = [sb(f"x_b{c}", [P, PACK * T], BF16) for c in range(4)]
+
+        def interleave(copy, dst, raw, a, b):
+            copy(
+                dst[:, PACK * a : PACK * b].rearrange("p (c i t) -> p c t i", i=4, t=4),
+                raw[:, :, a:b].rearrange("p t (c i) -> p c t i", i=4),
+            )
+
+        for c in range(4):
+            interleave(nc.vector.tensor_copy, x_b[c], x_raw[c], 0, X_VEC)
+            interleave(nc.scalar.copy, x_b[c], x_raw[c], X_VEC, T)
+            nc.vector.quantize_mx(out=x_q[c][:].bitcast(FP8X4), scales=x_s[c][:], in_=x_b[c][:])
+
+        def bank(i):
+            return psum.tile([P, T], F32, name=f"bank{i}")
+
+        acc = {}
+
+        def w_pass(i, c):
+            g, n = divmod(i, 4)
+            if c < 2:
+                lhs = w8_t[g][:, c, P * n : P * (n + 1)].bitcast(FP8X4)
+            else:
+                lhs = w4_t[g][:, c - 2, 2 * P * n : 2 * P * (n + 1)].bitcast(FP4X4)
+            if g == 0:
+                lhs_scale = planes0[:, c, P * n : P * (n + 1)]
+            else:
+                lhs_scale = planes1[:, c, P * i - G : P * (i + 1) - G]
+            nc.tensor.matmul_mx(
+                out=acc[i][:], lhsT=lhs, lhsT_scale=lhs_scale,
+                rhs=x_q[c][:].bitcast(FP8X4), rhs_scale=x_s[c][:], start=(c == 0), stop=False,
+            )
+
+        for i in range(4):
+            acc[i] = bank(i)
+        for c in range(4):
+            for i in range(4):
+                w_pass(i, c)
+
+        d_q = [sb(f"d_q{c}", [P, R], U32) for c in range(4)]
+        d_s = [sb(f"d_s{c}", [P, R], U8) for c in range(4)]
+        d_b = [sb(f"d_b{c}", [P, PACK * R], BF16) for c in range(3)]
+        d_bh = [sb(f"d_bh{i}", [P, PACK * R // 2], BF16) for i in range(2)]
+        h_acc = [bank(4 + t) for t in range(4)]
+
+        def permute(copy, dst, raw, a, b):
+            copy(
+                dst[:].rearrange("p (t m j) -> p m j t", t=4, j=4)[:, a:b],
+                raw[:].rearrange("p j (m t) -> p m j t", t=4)[:, a:b],
+            )
+
+        def h_pass(t, c):
+            cols = slice(P * t, P * (t + 1))
+            nc.tensor.matmul_mx(
+                out=h_acc[t][:], lhsT=d_q[c][:, cols].bitcast(FP8X4), lhsT_scale=d_s[c][:, cols],
+                rhs=x_q[c][:].bitcast(FP8X4), rhs_scale=x_s[c][:], start=(c == 0), stop=(c == 3),
+            )
+
+        for c in range(3):
+            permute(nc.vector.tensor_copy, d_b[c], d_raw[c], 0, D_VEC)
+            permute(nc.scalar.copy, d_b[c], d_raw[c], D_VEC, P)
+            nc.vector.quantize_mx(out=d_q[c][:].bitcast(FP8X4), scales=d_s[c][:], in_=d_b[c][:])
+            for t in range(4):
+                h_pass(t, c)
+        for i in range(2):
+            permute(nc.vector.tensor_copy, d_bh[i], d_raw_half[i], 0, D_VEC // 2)
+            permute(nc.scalar.copy, d_bh[i], d_raw_half[i], D_VEC // 2, P // 2)
+            for t in range(4):
+                cols = slice(P * t + 64 * i, P * t + 64 * (i + 1))
+                nc.vector.quantize_mx(
+                    out=d_q[3][:, cols].bitcast(FP8X4), scales=d_s[3][:, cols],
+                    in_=d_bh[i][:, 256 * t : 256 * (t + 1)],
+                )
+        for t in range(4):
+            h_pass(t, 3)
+
+        h_t = sb("h_t", [P, PACK, T], BF16)
+        h_b = sb("h_b", [P, PACK * T], BF16)
+        h_q = sb("h_q", [P, T], U32)
+        h_s = sb("h_s", [P, T], U8)
+        for t in range(4):
+            copy = nc.vector.tensor_copy if t % 2 else nc.scalar.copy
+            copy(h_t[:, t, :], h_acc[t][:])
+        interleave(nc.vector.tensor_copy, h_b, h_t, 0, H_VEC)
+        interleave(nc.scalar.copy, h_b, h_t, H_VEC, T)
+        nc.vector.quantize_mx(out=h_q[:].bitcast(FP8X4), scales=h_s[:], in_=h_b[:])
+
+        def up_pass(i):
+            nc.tensor.matmul_mx(
+                out=acc[i][:], lhsT=up_t[:, 2 * P * i : 2 * P * (i + 1)].bitcast(FP4X4),
+                lhsT_scale=up_plane[:, P * i : P * (i + 1)],
+                rhs=h_q[:].bitcast(FP8X4), rhs_scale=h_s[:], start=False, stop=True,
+            )
+            res = sb(f"res{i}", [P, T], F32)
+            copy = nc.scalar.copy if i % 2 else nc.vector.tensor_copy
+            copy(res[:], acc[i][:])
+            nc.sync.dma_start(out=out[P * i : P * (i + 1), :], in_=res[:])
+
+        for i in range(4, 8):
+            acc[i] = bank(i)
+        for c in range(2):
+            for i in range(4, 8):
+                w_pass(i, c)
+        for i in range(4):
+            up_pass(i)
+        for i in range(4, 8):
+            w_pass(i, 2)
+            w_pass(i, 3)
+            up_pass(i)
+        for i in range(8, 12):
+            acc[i] = bank(i - 8)
+            for c in range(4):
+                w_pass(i, c)
+            up_pass(i)

@@ -33,8 +33,8 @@ def tile_mix_three_fm_none_kernel(
         def sb(name, shape, dtype):
             return keep.tile(shape, dtype, name=name, align_bytes=64)
 
-        planes0 = sb("planes0", [P, 4, G], U8)
-        planes1 = sb("planes1", [P, 4, M - G], U8)
+        planes0 = sb("planes0", [P, 4, 2 * G], U8)
+        planes1 = sb("planes1", [P, 4, G], U8)
         up_plane = sb("up_plane", [P, M], U8)
         warm_in = sb("warm_in", [P, 1], F32)
         warm_out = sb("warm_out", [P, 1], F32)
@@ -71,26 +71,26 @@ def tile_mix_three_fm_none_kernel(
         load_k(x_raw[0], x, 0, slice(0, T))
         load_k(x_raw[1], x, 1, slice(0, T))
         for r in range(4):
-            load_scales(nc.sync, planes0[:, 0:2, :], w8_rows, r, slice(0, G))
+            load_scales(nc.sync, planes0[:, 0:2, :], w8_rows, r, slice(0, 2 * G))
         load_k(x_raw[2], x, 2, slice(0, T))
         load_k(x_raw[3], x, 3, slice(0, T))
         for r in range(2):
-            load_scales(nc.sync, planes0[:, 2:4, :], w4_rows, r, slice(0, G))
+            load_scales(nc.sync, planes0[:, 2:4, :], w4_rows, r, slice(0, 2 * G))
         load_w(0)
         for r in range(2, 4):
-            load_scales(nc.sync, planes0[:, 2:4, :], w4_rows, r, slice(0, G))
+            load_scales(nc.sync, planes0[:, 2:4, :], w4_rows, r, slice(0, 2 * G))
         for c in range(3):
             load_k(d_raw[c], down, c, slice(0, R))
         for i in range(2):
             load_k(d_raw_half[i], down, 3, slice(256 * i, 256 * (i + 1)))
         load_w(1)
-        for r in range(4):
-            load_scales(nc.sync, planes1[:, 0:2, :], w8_rows, r, slice(G, M))
-        for r in range(4):
-            load_scales(nc.sync, planes1[:, 2:4, :], w4_rows, r, slice(G, M))
+        nc.sync.dma_start(out=up_t[:].bitcast(I32), in_=up_words[0].bitcast(I32))
         for r in range(4):
             nc.sync.dma_start(out=up_plane[r:P:32, :].bitcast(I32), in_=up_rows[r][:, 0, :].bitcast(I32))
-        nc.sync.dma_start(out=up_t[:].bitcast(I32), in_=up_words[0].bitcast(I32))
+        for r in range(4):
+            load_scales(nc.sync, planes1[:, 0:2, :], w8_rows, r, slice(2 * G, M))
+        for r in range(4):
+            load_scales(nc.sync, planes1[:, 2:4, :], w4_rows, r, slice(2 * G, M))
         load_w(2)
 
         x_q = [sb(f"x_q{c}", [P, T], U32) for c in range(4)]
@@ -119,10 +119,10 @@ def tile_mix_three_fm_none_kernel(
                 lhs = w8_t[g][:, c, P * n : P * (n + 1)].bitcast(FP8X4)
             else:
                 lhs = w4_t[g][:, c - 2, 2 * P * n : 2 * P * (n + 1)].bitcast(FP4X4)
-            if g == 0:
-                lhs_scale = planes0[:, c, P * n : P * (n + 1)]
+            if g < 2:
+                lhs_scale = planes0[:, c, P * i : P * (i + 1)]
             else:
-                lhs_scale = planes1[:, c, P * i - G : P * (i + 1) - G]
+                lhs_scale = planes1[:, c, P * n : P * (n + 1)]
             nc.tensor.matmul_mx(
                 out=acc[i][:], lhsT=lhs, lhsT_scale=lhs_scale,
                 rhs=x_q[c][:].bitcast(FP8X4), rhs_scale=x_s[c][:], start=(c == 0), stop=False,
@@ -195,14 +195,10 @@ def tile_mix_three_fm_none_kernel(
 
         for i in range(4, 8):
             acc[i] = bank(i)
-        for c in range(2):
+        for c in range(4):
             for i in range(4, 8):
                 w_pass(i, c)
-        for i in range(4):
-            up_pass(i)
-        for i in range(4, 8):
-            w_pass(i, 2)
-            w_pass(i, 3)
+        for i in range(8):
             up_pass(i)
         for i in range(8, 12):
             acc[i] = bank(i - 8)

@@ -16,8 +16,8 @@ FP4X4 = mybir.dt.float4_e2m1fn_x4
 P = 128
 PACK = 4
 G = 512
-X_VEC = 336
-D_VEC = 88
+X_VEC = 288
+D_VEC = 80
 H_VEC = 344
 
 
@@ -31,10 +31,10 @@ def tile_mix_three_fm_none_kernel(
         ctx.enter_context(tc.manual_schedule())
 
         def sb(name, shape, dtype):
-            return keep.tile(shape, dtype, name=name, align_bytes=64)
+            return keep.tile(shape, dtype, name=name, align_bytes=256)
 
-        planes0 = sb("planes0", [P, 4, 2 * G], U8)
-        planes1 = sb("planes1", [P, 4, G], U8)
+        planes0 = sb("planes0", [P, 4, G], U8)
+        planes1 = sb("planes1", [P, 4, M - G], U8)
         up_plane = sb("up_plane", [P, M], U8)
         warm_in = sb("warm_in", [P, 1], F32)
         warm_out = sb("warm_out", [P, 1], F32)
@@ -50,6 +50,11 @@ def tile_mix_three_fm_none_kernel(
 
         def load_scales(queue, plane, rows, r, cols):
             queue.dma_start(out=plane[r:P:32].bitcast(I32), in_=rows[r][:, :, cols].bitcast(I32))
+
+        for r in range(4):
+            load_scales(nc.gpsimd, planes0[:, 0:2, :], w8_rows, r, slice(0, G))
+        for r in range(4):
+            load_scales(nc.gpsimd, planes0[:, 2:4, :], w4_rows, r, slice(0, G))
 
         x_raw = [sb(f"x_raw{c}", [P, PACK, T], F32) for c in range(4)]
         d_raw = [sb(f"d_raw{c}", [P, PACK, R], F32) for c in range(3)]
@@ -70,27 +75,21 @@ def tile_mix_three_fm_none_kernel(
 
         load_k(x_raw[0], x, 0, slice(0, T))
         load_k(x_raw[1], x, 1, slice(0, T))
-        for r in range(4):
-            load_scales(nc.sync, planes0[:, 0:2, :], w8_rows, r, slice(0, 2 * G))
         load_k(x_raw[2], x, 2, slice(0, T))
         load_k(x_raw[3], x, 3, slice(0, T))
-        for r in range(2):
-            load_scales(nc.sync, planes0[:, 2:4, :], w4_rows, r, slice(0, 2 * G))
         load_w(0)
-        for r in range(2, 4):
-            load_scales(nc.sync, planes0[:, 2:4, :], w4_rows, r, slice(0, 2 * G))
         for c in range(3):
             load_k(d_raw[c], down, c, slice(0, R))
         for i in range(2):
             load_k(d_raw_half[i], down, 3, slice(256 * i, 256 * (i + 1)))
         load_w(1)
+        for r in range(4):
+            load_scales(nc.sync, planes1[:, 0:2, :], w8_rows, r, slice(G, M))
+        for r in range(4):
+            load_scales(nc.sync, planes1[:, 2:4, :], w4_rows, r, slice(G, M))
         nc.sync.dma_start(out=up_t[:].bitcast(I32), in_=up_words[0].bitcast(I32))
         for r in range(4):
             nc.sync.dma_start(out=up_plane[r:P:32, :].bitcast(I32), in_=up_rows[r][:, 0, :].bitcast(I32))
-        for r in range(4):
-            load_scales(nc.sync, planes1[:, 0:2, :], w8_rows, r, slice(2 * G, M))
-        for r in range(4):
-            load_scales(nc.sync, planes1[:, 2:4, :], w4_rows, r, slice(2 * G, M))
         load_w(2)
 
         x_q = [sb(f"x_q{c}", [P, T], U32) for c in range(4)]
@@ -119,10 +118,10 @@ def tile_mix_three_fm_none_kernel(
                 lhs = w8_t[g][:, c, P * n : P * (n + 1)].bitcast(FP8X4)
             else:
                 lhs = w4_t[g][:, c - 2, 2 * P * n : 2 * P * (n + 1)].bitcast(FP4X4)
-            if g < 2:
-                lhs_scale = planes0[:, c, P * i : P * (i + 1)]
+            if g == 0:
+                lhs_scale = planes0[:, c, P * n : P * (n + 1)]
             else:
-                lhs_scale = planes1[:, c, P * n : P * (n + 1)]
+                lhs_scale = planes1[:, c, P * i - G : P * (i + 1) - G]
             nc.tensor.matmul_mx(
                 out=acc[i][:], lhsT=lhs, lhsT_scale=lhs_scale,
                 rhs=x_q[c][:].bitcast(FP8X4), rhs_scale=x_s[c][:], start=(c == 0), stop=False,
@@ -130,7 +129,7 @@ def tile_mix_three_fm_none_kernel(
 
         for i in range(4):
             acc[i] = bank(i)
-        for c in range(4):
+        for c in range(2):
             for i in range(4):
                 w_pass(i, c)
 
@@ -159,6 +158,9 @@ def tile_mix_three_fm_none_kernel(
             nc.vector.quantize_mx(out=d_q[c][:].bitcast(FP8X4), scales=d_s[c][:], in_=d_b[c][:])
             for t in range(4):
                 h_pass(t, c)
+            if c:
+                for i in range(4):
+                    w_pass(i, c + 1)
         for i in range(2):
             permute(nc.vector.tensor_copy, d_bh[i], d_raw_half[i], 0, D_VEC // 2)
             permute(nc.scalar.copy, d_bh[i], d_raw_half[i], D_VEC // 2, P // 2)

@@ -112,8 +112,9 @@ def tile_mix_three_fm_none_kernel(
 
         acc = {}
 
-        def w_pass(i, c):
+        def w_pass(i, c, tile=None, cols=slice(0, T)):
             g, n = divmod(i, 4)
+            tile = acc[i] if tile is None else tile
             if c < 2:
                 lhs = w8_t[g][:, c, P * n : P * (n + 1)].bitcast(FP8X4)
             else:
@@ -123,8 +124,8 @@ def tile_mix_three_fm_none_kernel(
             else:
                 lhs_scale = planes1[:, c, P * i - G : P * (i + 1) - G]
             nc.tensor.matmul_mx(
-                out=acc[i][:], lhsT=lhs, lhsT_scale=lhs_scale,
-                rhs=x_q[c][:].bitcast(FP8X4), rhs_scale=x_s[c][:], start=(c == 0), stop=False,
+                out=tile[:], lhsT=lhs, lhsT_scale=lhs_scale,
+                rhs=x_q[c][:, cols].bitcast(FP8X4), rhs_scale=x_s[c][:, cols], start=(c == 0), stop=False,
             )
 
         for i in range(4):
@@ -184,16 +185,18 @@ def tile_mix_three_fm_none_kernel(
         interleave(nc.scalar.copy, h_b, h_t, H_VEC, T)
         nc.vector.quantize_mx(out=h_q[:].bitcast(FP8X4), scales=h_s[:], in_=h_b[:])
 
-        def up_pass(i):
+        def up_pass(i, tile=None, cols=slice(0, T), on_scalar=None):
+            tile = acc[i] if tile is None else tile
+            on_scalar = i % 2 if on_scalar is None else on_scalar
             nc.tensor.matmul_mx(
-                out=acc[i][:], lhsT=up_t[:, 2 * P * i : 2 * P * (i + 1)].bitcast(FP4X4),
+                out=tile[:], lhsT=up_t[:, 2 * P * i : 2 * P * (i + 1)].bitcast(FP4X4),
                 lhsT_scale=up_plane[:, P * i : P * (i + 1)],
-                rhs=h_q[:].bitcast(FP8X4), rhs_scale=h_s[:], start=False, stop=True,
+                rhs=h_q[:, cols].bitcast(FP8X4), rhs_scale=h_s[:, cols], start=False, stop=True,
             )
-            res = sb(f"res{i}", [P, T], F32)
-            copy = nc.scalar.copy if i % 2 else nc.vector.tensor_copy
-            copy(res[:], acc[i][:])
-            nc.sync.dma_start(out=out[P * i : P * (i + 1), :], in_=res[:])
+            res = sb(f"res{i}_{cols.start}", [P, cols.stop - cols.start], F32)
+            copy = nc.scalar.copy if on_scalar else nc.vector.tensor_copy
+            copy(res[:], tile[:])
+            nc.sync.dma_start(out=out[P * i : P * (i + 1), cols], in_=res[:])
 
         for i in range(4, 8):
             acc[i] = bank(i)
@@ -202,8 +205,14 @@ def tile_mix_three_fm_none_kernel(
                 w_pass(i, c)
         for i in range(8):
             up_pass(i)
-        for i in range(8, 12):
+        for i in range(8, 11):
             acc[i] = bank(i - 8)
             for c in range(4):
                 w_pass(i, c)
             up_pass(i)
+        for q in range(4):
+            cols = slice(P * q, P * (q + 1))
+            tile = psum.tile([P, P], F32, name=f"bank{3 + q}")
+            for c in range(4):
+                w_pass(11, c, tile, cols)
+            up_pass(11, tile, cols, q % 2 == 0)

@@ -58,30 +58,30 @@ def tile_mix_three_fm_none_kernel(
 
         x_raw = [sb(f"x_raw{c}", [P, PACK, T], F32) for c in range(4)]
         d_raw = [sb(f"d_raw{c}", [P, PACK, R], F32) for c in range(3)]
-        d_raw_half = [sb(f"d_rawh{i}", [P, PACK, R // 2], F32) for i in range(2)]
+        d_raw_half = [sb(f"d_rawh{i}", [P, 2, R], F32) for i in range(2)]
         w8_t = [sb(f"w8_{g}", [P, 2, G], U32) for g in range(3)]
         w4_t = [sb(f"w4_{g}", [P, 2, 2 * G], U8) for g in range(3)]
         up_t = sb("up_t", [P, 2 * M], U8)
         w8_view = w8_words.rearrange("a p n i -> p a (n i)")
         w4_view = w4_words.rearrange("a p b -> p a b")
 
-        def load_k(tile, src, c, cols):
+        def load_k(tile, src, c, j0=0, j1=PACK):
             rows = src[512 * c : 512 * (c + 1), :].rearrange("(p j) w -> p j w", j=PACK)
-            nc.sync.dma_start(out=tile[:], in_=rows[:, :, cols])
+            nc.sync.dma_start(out=tile[:], in_=rows[:, j0:j1, :])
 
         def load_w(g):
             nc.sync.dma_start(out=w8_t[g][:].bitcast(I32), in_=w8_view[:, :, 4 * G * g : 4 * G * (g + 1)].bitcast(I32))
             nc.sync.dma_start(out=w4_t[g][:].bitcast(I32), in_=w4_view[:, :, 2 * G * g : 2 * G * (g + 1)].bitcast(I32))
 
-        load_k(x_raw[0], x, 0, slice(0, T))
-        load_k(x_raw[1], x, 1, slice(0, T))
-        load_k(x_raw[2], x, 2, slice(0, T))
-        load_k(x_raw[3], x, 3, slice(0, T))
+        load_k(x_raw[0], x, 0)
+        load_k(x_raw[1], x, 1)
+        load_k(x_raw[2], x, 2)
+        load_k(x_raw[3], x, 3)
         load_w(0)
         for c in range(3):
-            load_k(d_raw[c], down, c, slice(0, R))
+            load_k(d_raw[c], down, c)
         for i in range(2):
-            load_k(d_raw_half[i], down, 3, slice(256 * i, 256 * (i + 1)))
+            load_k(d_raw_half[i], down, 3, 2 * i, 2 * i + 2)
         load_w(1)
         for r in range(4):
             load_scales(nc.sync, planes1[:, 0:2, :], w8_rows, r, slice(G, M))
@@ -136,13 +136,12 @@ def tile_mix_three_fm_none_kernel(
 
         d_q = [sb(f"d_q{c}", [P, R], U32) for c in range(4)]
         d_s = [sb(f"d_s{c}", [P, R], U8) for c in range(4)]
-        d_b = [sb(f"d_b{c}", [P, PACK * R], BF16) for c in range(3)]
-        d_bh = [sb(f"d_bh{i}", [P, PACK * R // 2], BF16) for i in range(2)]
+        d_b = [sb(f"d_b{c}", [P, PACK * R], BF16) for c in range(4)]
         h_acc = [bank(4 + t) for t in range(4)]
 
-        def permute(copy, dst, raw, a, b):
+        def permute(copy, dst, raw, a, b, j0=0, j1=PACK):
             copy(
-                dst[:].rearrange("p (t m j) -> p m j t", t=4, j=4)[:, a:b],
+                dst[:].rearrange("p (t m j) -> p m j t", t=4, j=4)[:, a:b, j0:j1],
                 raw[:].rearrange("p j (m t) -> p m j t", t=4)[:, a:b],
             )
 
@@ -159,19 +158,18 @@ def tile_mix_three_fm_none_kernel(
             nc.vector.quantize_mx(out=d_q[c][:].bitcast(FP8X4), scales=d_s[c][:], in_=d_b[c][:])
             for t in range(4):
                 h_pass(t, c)
-            if c:
+            if c < 2:
                 for i in range(4):
-                    w_pass(i, c + 1)
+                    w_pass(i, c + 2)
         for i in range(2):
-            permute(nc.vector.tensor_copy, d_bh[i], d_raw_half[i], 0, D_VEC // 2)
-            permute(nc.scalar.copy, d_bh[i], d_raw_half[i], D_VEC // 2, P // 2)
-            for t in range(4):
-                cols = slice(P * t + 64 * i, P * t + 64 * (i + 1))
-                nc.vector.quantize_mx(
-                    out=d_q[3][:, cols].bitcast(FP8X4), scales=d_s[3][:, cols],
-                    in_=d_bh[i][:, 256 * t : 256 * (t + 1)],
-                )
+            permute(nc.vector.tensor_copy, d_b[3], d_raw_half[i], 0, D_VEC, 2 * i, 2 * i + 2)
+            permute(nc.scalar.copy, d_b[3], d_raw_half[i], D_VEC, P, 2 * i, 2 * i + 2)
         for t in range(4):
+            cols = slice(P * t, P * (t + 1))
+            nc.vector.quantize_mx(
+                out=d_q[3][:, cols].bitcast(FP8X4), scales=d_s[3][:, cols],
+                in_=d_b[3][:, 512 * t : 512 * (t + 1)],
+            )
             h_pass(t, 3)
 
         h_t = sb("h_t", [P, PACK, T], BF16)
@@ -215,4 +213,4 @@ def tile_mix_three_fm_none_kernel(
             tile = psum.tile([P, P], F32, name=f"bank{3 + q}")
             for c in range(4):
                 w_pass(11, c, tile, cols)
-            up_pass(11, tile, cols, q % 2 == 0)
+            up_pass(11, tile, cols, q % 2)

from contextlib import ExitStack

import concourse.mybir as mybir

K, T, R, M = 2048, 512, 512, 1536
FLOPS = 2 * (K * R * T + K * M * T + R * M * T)

F32 = mybir.dt.float32
BF16 = mybir.dt.bfloat16
I32 = mybir.dt.int32
U32 = mybir.dt.uint32
U8 = mybir.dt.uint8
FP8X4 = mybir.dt.float8_e4m3fn_x4
FP4X4 = mybir.dt.float4_e2m1fn_x4

P = 128
PACK = 4
G = 512
X_VEC = 288
D_VEC = 80
H_VEC = 344


def tile_mix_three_fm_none_kernel(
    tc, x, w8_words, w8_scales, w4_words, w4_scales, down, up_words, up_scales, out
):
    nc = tc.nc
    with ExitStack() as ctx:
        keep = ctx.enter_context(tc.tile_pool(name="keep", bufs=1))
        psum = ctx.enter_context(tc.psum_pool(name="psum", bufs=1))
        ctx.enter_context(tc.manual_schedule())

        def sb(name, shape, dtype):
            return keep.tile(shape, dtype, name=name, align_bytes=256)

        planes0 = sb("planes0", [P, 4, G], U8)
        planes1 = sb("planes1", [P, 4, M - G], U8)
        up_plane = sb("up_plane", [P, M], U8)
        warm_in = sb("warm_in", [P, 1], F32)
        warm_out = sb("warm_out", [P, 1], F32)
        nc.vector.memset(planes0[:].rearrange("p a n -> p (a n)").bitcast(I32), 0)
        nc.vector.memset(warm_in[:], 0.0)
        nc.vector.memset(planes1[:].rearrange("p a n -> p (a n)").bitcast(I32), 0)
        nc.vector.memset(up_plane[:].bitcast(I32), 0)
        nc.scalar.copy(warm_out[:], warm_in[:])

        w8_rows = w8_scales.rearrange("a (q r) n -> r q a n", r=4)
        w4_rows = w4_scales.rearrange("a (q r) n -> r q a n", r=4)
        up_rows = up_scales.rearrange("a (q r) n -> r q a n", r=4)

        def load_scales(queue, plane, rows, r, cols):
            queue.dma_start(out=plane[r:P:32].bitcast(I32), in_=rows[r][:, :, cols].bitcast(I32))

        for r in range(4):
            load_scales(nc.gpsimd, planes0[:, 0:2, :], w8_rows, r, slice(0, G))
        for r in range(4):
            load_scales(nc.gpsimd, planes0[:, 2:4, :], w4_rows, r, slice(0, G))

        x_raw = [sb(f"x_raw{c}", [P, PACK, T], F32) for c in range(4)]
        d_raw = [sb(f"d_raw{c}", [P, PACK, R], F32) for c in range(3)]
        d_raw_half = [sb(f"d_rawh{i}", [P, 2, R], F32) for i in range(2)]
        w8_t = [sb(f"w8_{g}", [P, 2, G], U32) for g in range(3)]
        w4_t = [sb(f"w4_{g}", [P, 2, 2 * G], U8) for g in range(3)]
        up_t = sb("up_t", [P, 2 * M], U8)
        w8_view = w8_words.rearrange("a p n i -> p a (n i)")
        w4_view = w4_words.rearrange("a p b -> p a b")

        def load_k(tile, src, c, j0=0, j1=PACK):
            rows = src[512 * c : 512 * (c + 1), :].rearrange("(p j) w -> p j w", j=PACK)
            nc.sync.dma_start(out=tile[:], in_=rows[:, j0:j1, :])

        def load_w(g):
            nc.sync.dma_start(out=w8_t[g][:].bitcast(I32), in_=w8_view[:, :, 4 * G * g : 4 * G * (g + 1)].bitcast(I32))
            nc.sync.dma_start(out=w4_t[g][:].bitcast(I32), in_=w4_view[:, :, 2 * G * g : 2 * G * (g + 1)].bitcast(I32))

        load_k(x_raw[0], x, 0)
        load_k(x_raw[1], x, 1)
        load_k(x_raw[2], x, 2)
        load_k(x_raw[3], x, 3)
        load_w(0)
        for c in range(3):
            load_k(d_raw[c], down, c)
        for i in range(2):
            load_k(d_raw_half[i], down, 3, 2 * i, 2 * i + 2)
        load_w(1)
        for r in range(4):
            load_scales(nc.sync, planes1[:, 0:2, :], w8_rows, r, slice(G, M))
        for r in range(4):
            load_scales(nc.sync, planes1[:, 2:4, :], w4_rows, r, slice(G, M))
        nc.sync.dma_start(out=up_t[:].bitcast(I32), in_=up_words[0].bitcast(I32))
        for r in range(4):
            nc.sync.dma_start(out=up_plane[r:P:32, :].bitcast(I32), in_=up_rows[r][:, 0, :].bitcast(I32))
        load_w(2)

        x_q = [sb(f"x_q{c}", [P, T], U32) for c in range(4)]
        x_s = [sb(f"x_s{c}", [P, T], U8) for c in range(4)]
        x_b = [sb(f"x_b{c}", [P, PACK * T], BF16) for c in range(4)]

        def interleave(copy, dst, raw, a, b):
            copy(
                dst[:, PACK * a : PACK * b].rearrange("p (c i t) -> p c t i", i=4, t=4),
                raw[:, :, a:b].rearrange("p t (c i) -> p c t i", i=4),
            )

        for c in range(4):
            interleave(nc.vector.tensor_copy, x_b[c], x_raw[c], 0, X_VEC)
            interleave(nc.scalar.copy, x_b[c], x_raw[c], X_VEC, T)
            nc.vector.quantize_mx(out=x_q[c][:].bitcast(FP8X4), scales=x_s[c][:], in_=x_b[c][:])

        def bank(i):
            return psum.tile([P, T], F32, name=f"bank{i}")

        acc = {}

        def w_pass(i, c, tile=None, cols=slice(0, T)):
            g, n = divmod(i, 4)
            tile = acc[i] if tile is None else tile
            if c < 2:
                lhs = w8_t[g][:, c, P * n : P * (n + 1)].bitcast(FP8X4)
            else:
                lhs = w4_t[g][:, c - 2, 2 * P * n : 2 * P * (n + 1)].bitcast(FP4X4)
            if g == 0:
                lhs_scale = planes0[:, c, P * n : P * (n + 1)]
            else:
                lhs_scale = planes1[:, c, P * i - G : P * (i + 1) - G]
            nc.tensor.matmul_mx(
                out=tile[:], lhsT=lhs, lhsT_scale=lhs_scale,
                rhs=x_q[c][:, cols].bitcast(FP8X4), rhs_scale=x_s[c][:, cols], start=(c == 0), stop=False,
            )

        for i in range(4):
            acc[i] = bank(i)
        for c in range(2):
            for i in range(4):
                w_pass(i, c)

        d_q = [sb(f"d_q{c}", [P, R], U32) for c in range(4)]
        d_s = [sb(f"d_s{c}", [P, R], U8) for c in range(4)]
        d_b = [sb(f"d_b{c}", [P, PACK * R], BF16) for c in range(4)]
        h_acc = [bank(4 + t) for t in range(4)]

        def permute(copy, dst, raw, a, b, j0=0, j1=PACK):
            copy(
                dst[:].rearrange("p (t m j) -> p m j t", t=4, j=4)[:, a:b, j0:j1],
                raw[:].rearrange("p j (m t) -> p m j t", t=4)[:, a:b],
            )

        def h_pass(t, c):
            cols = slice(P * t, P * (t + 1))
            nc.tensor.matmul_mx(
                out=h_acc[t][:], lhsT=d_q[c][:, cols].bitcast(FP8X4), lhsT_scale=d_s[c][:, cols],
                rhs=x_q[c][:].bitcast(FP8X4), rhs_scale=x_s[c][:], start=(c == 0), stop=(c == 3),
            )

        for c in range(3):
            permute(nc.vector.tensor_copy, d_b[c], d_raw[c], 0, D_VEC)
            permute(nc.scalar.copy, d_b[c], d_raw[c], D_VEC, P)
            nc.vector.quantize_mx(out=d_q[c][:].bitcast(FP8X4), scales=d_s[c][:], in_=d_b[c][:])
            for t in range(4):
                h_pass(t, c)
            if c < 2:
                for i in range(4):
                    w_pass(i, c + 2)
        for i in range(2):
            permute(nc.vector.tensor_copy, d_b[3], d_raw_half[i], 0, D_VEC, 2 * i, 2 * i + 2)
            permute(nc.scalar.copy, d_b[3], d_raw_half[i], D_VEC, P, 2 * i, 2 * i + 2)
        for t in range(4):
            cols = slice(P * t, P * (t + 1))
            nc.vector.quantize_mx(
                out=d_q[3][:, cols].bitcast(FP8X4), scales=d_s[3][:, cols],
                in_=d_b[3][:, 512 * t : 512 * (t + 1)],
            )
            h_pass(t, 3)

        h_t = sb("h_t", [P, PACK, T], BF16)
        h_b = sb("h_b", [P, PACK * T], BF16)
        h_q = sb("h_q", [P, T], U32)
        h_s = sb("h_s", [P, T], U8)
        for t in range(4):
            copy = nc.vector.tensor_copy if t % 2 else nc.scalar.copy
            copy(h_t[:, t, :], h_acc[t][:])
        interleave(nc.vector.tensor_copy, h_b, h_t, 0, H_VEC)
        interleave(nc.scalar.copy, h_b, h_t, H_VEC, T)
        nc.vector.quantize_mx(out=h_q[:].bitcast(FP8X4), scales=h_s[:], in_=h_b[:])

        def up_pass(i, tile=None, cols=slice(0, T), on_scalar=None):
            tile = acc[i] if tile is None else tile
            on_scalar = i % 2 if on_scalar is None else on_scalar
            nc.tensor.matmul_mx(
                out=tile[:], lhsT=up_t[:, 2 * P * i : 2 * P * (i + 1)].bitcast(FP4X4),
                lhsT_scale=up_plane[:, P * i : P * (i + 1)],
                rhs=h_q[:, cols].bitcast(FP8X4), rhs_scale=h_s[:, cols], start=False, stop=True,
            )
            res = sb(f"res{i}_{cols.start}", [P, cols.stop - cols.start], F32)
            copy = nc.scalar.copy if on_scalar else nc.vector.tensor_copy
            copy(res[:], tile[:])
            nc.sync.dma_start(out=out[P * i : P * (i + 1), cols], in_=res[:])

        for i in range(4, 8):
            acc[i] = bank(i)
        for c in range(4):
            for i in range(4, 8):
                w_pass(i, c)
        for i in range(8):
            up_pass(i)
        for i in range(8, 11):
            acc[i] = bank(i - 8)
            for c in range(4):
                w_pass(i, c)
            up_pass(i)
        for q in range(4):
            cols = slice(P * q, P * (q + 1))
            tile = psum.tile([P, P], F32, name=f"bank{3 + q}")
            for c in range(4):
                w_pass(11, c, tile, cols)
            up_pass(11, tile, cols, q % 2)
